import numpy as np
import ml_dtypes


def mxq(x, axis, fmt="e4m3"):
    dtype, down = {"e4m3": (ml_dtypes.float8_e4m3fn, 7), "e5m2": (ml_dtypes.float8_e5m2, 14)}[fmt]
    v = np.moveaxis(np.asarray(x, np.float32).astype(ml_dtypes.bfloat16).astype(np.float64), axis, -1)
    blocks = v.reshape(v.shape[:-1] + (-1, 32))
    amax = np.abs(blocks).max(-1, keepdims=True)
    byte = np.maximum(np.where(amax > 0, np.frexp(amax)[1] - 1 + 127, 0) - down, 1)
    scale = np.exp2(byte - 127.0)
    codes = (blocks / scale).astype(np.float32).astype(dtype).astype(np.float64)
    return np.moveaxis((codes * scale).reshape(v.shape), -1, axis)


WIDE = False


def mx_kscale(k):
    if not WIDE:
        return np.ones(k)
    levels = np.array([10, -10, 5, -5, 0])
    if k % 512:
        return np.exp2(np.random.permutation(np.resize(levels, k // 32))).repeat(32)
    a = np.empty((k // 512, 16))
    for p in range(k // 512):
        a[p, :8] = np.random.permutation(np.resize(levels, 8))
        for g in range(8):
            far = levels[np.abs(levels - a[p, g]) >= 10]
            a[p, g + 8] = far[np.random.randint(len(far))]
    return np.exp2(a.ravel()).repeat(32)


def f64(x):
    return np.asarray(x).astype(np.float64)


def striped(idx):
    return np.tile(np.asarray(idx).reshape(-1, 16).T, (8, 1)).astype(np.uint16)


def unstriped(offs):
    return offs[:16].T.reshape(-1).astype(np.int64)


G, K, T, D, M = 256, 4, 4096, 512, 384


def setup_inputs():
    n = np.random.standard_normal
    s = mx_kscale(D)[:, None]
    grid = lambda x: np.round(x * 32) / 32
    x = grid(n((D, T))) * s
    idx = np.random.randint(0, T, (G, K))
    part = np.random.randint(1, 128 // K, (G, K)) / 64.0
    return {
        "xT": x.astype(np.float32),
        "w": (n((D, M)) / np.sqrt(D) / s).astype(np.float32),
        "part": np.tile(part.reshape(-1), (128, 1)).astype(np.float32),
        "bias": (0.3 * n((M, 1))).astype(np.float32),
        "offs": striped(idx.reshape(-1)),
    }


def reference(xT, w, part, bias, offs):
    x = f64(xT)[:, unstriped(offs)]
    y = mxq(f64(w), 0, "e4m3").T @ mxq((x * f64(part)[:1]).reshape(D, G, K).sum(-1), 0, "e4m3")
    y = y + f64(bias)
    return y

@@ -1,0 +1,112 @@
+from contextlib import ExitStack
+
+import concourse.mybir as mybir
+from concourse.masks import make_identity
+
+D, T, M, G, K = 512, 4096, 384, 256, 4
+P, PACK = 128, 4
+HALF = 128
+MB = M // P
+
+F32 = mybir.dt.float32
+BF16 = mybir.dt.bfloat16
+U32 = mybir.dt.uint32
+U16 = mybir.dt.uint16
+U8 = mybir.dt.uint8
+X4 = mybir.dt.float8_e4m3fn_x4
+ADD = mybir.AluOpType.add
+MULT = mybir.AluOpType.mult
+AX = mybir.AxisListType.X
+IDENT = mybir.ActivationFunctionType.Identity
+
+FLOPS = 2 * D * M * G
+BYTES = 4 * (D * T + D * M + G * K + M + M * G) + 2 * P * (G * K // 16)
+
+
+def tile_attend_grid_bias_kernel(tc, xT, w, part, bias, offs, out):
+    nc = tc.nc
+    x_planes = xT.rearrange("(p t) c -> t p c", t=PACK)
+    w_planes = w.rearrange("(p t) m -> p t m", t=PACK)
+    out_rows = out.rearrange("(q b) g -> q b g", b=MB)
+    with ExitStack() as ctx:
+        ctx.enter_context(nc.allow_low_precision("sums are rounded once to bfloat16"))
+        lists = ctx.enter_context(tc.tile_pool(name="lists", bufs=1))
+        keep = ctx.enter_context(tc.tile_pool(name="keep", bufs=1))
+        ring = ctx.enter_context(tc.tile_pool(name="ring", bufs=2))
+        psum = ctx.enter_context(tc.psum_pool(name="psum", bufs=1))
+
+        offsets = lists.tile([P, G * K // 16], U16, name="offsets")
+        part_col = keep.tile([P, 8], F32, name="part_col")
+        bias_col = keep.tile([P, MB], F32, name="bias_col")
+        x_sb = [keep.tile([P, T], F32, name=f"x{t}") for t in range(PACK)]
+        w_sb = [keep.tile([P, PACK, M // 2], F32, name=f"w{c}") for c in range(2)]
+
+        nc.sync.dma_start(part_col[:], part[0:1, :].rearrange("o (p j) -> (o p) j", j=8))
+        nc.sync.dma_start(x_sb[0][:], x_planes[0])
+        nc.sync.dma_start(offsets[:], offs)
+        nc.scalar.dma_start(bias_col[:], bias.rearrange("(q b) o -> q (b o)", b=MB))
+        for t in range(1, PACK):
+            nc.sync.dma_start(x_sb[t][:], x_planes[t])
+        for c in range(2):
+            nc.sync.dma_start(w_sb[c][:], w_planes[:, :, c * (M // 2) : (c + 1) * (M // 2)])
+
+        ident = keep.tile([P, P], F32, name="ident")
+        make_identity(nc, ident[:])
+        part_sb = keep.tile([P, P, 8], F32, name="part_sb")
+        for h in range(2):
+            pt = psum.tile([P, 4, P], F32, name=f"pt{h}")
+            for j in range(4):
+                nc.tensor.transpose(pt[:, j, :], part_col[:, 4 * h + j : 4 * h + j + 1].to_broadcast([P, P]), ident[:])
+            nc.scalar.copy(out=part_sb[:, :, 4 * h : 4 * h + 4], in_=pt[:].rearrange("p j a -> p a j"))
+        part_row = part_sb[:].rearrange("p a j -> p (a j)")
+
+        e = keep.tile([P, G, PACK], BF16, name="e", align_bytes=64)
+        for t in range(PACK - 1):
+            prod = ring.tile([P, G * K], F32, name="prod")
+            nc.vector.tensor_tensor(prod[:], x_sb[t][:].indirect(offsets[:]), part_row, MULT)
+            nc.vector.tensor_reduce(e[:, :, t], prod[:].rearrange("p (g k) -> p g k", k=K), AX, ADD)
+
+        w_grouped = keep.tile([P, MB, P, PACK], BF16, name="w_grouped", align_bytes=64)
+        w_codes = keep.tile([P, MB, P], U32, name="w_codes", align_bytes=64)
+        w_scales = keep.tile([P, MB, P], U8, name="w_scales", align_bytes=64)
+        e_codes = keep.tile([P, G], U32, name="e_codes", align_bytes=64)
+        e_scales = keep.tile([P, G], U8, name="e_scales", align_bytes=64)
+        t = PACK - 1
+        last = [ring.tile([P, HALF * K], F32, name=f"last{h}") for h in range(2)]
+        for h in range(2):
+            n = HALF * K
+            nc.vector.tensor_tensor(last[h][:], x_sb[t][:].indirect(offsets[:, h * n // 16 : (h + 1) * n // 16]), part_row[:, h * n : (h + 1) * n], MULT)
+        for c in range(2):
+            nc.scalar.copy(out=w_grouped[:, :, 64 * c : 64 * c + 64, :], in_=w_sb[c][:].rearrange("p t (q b) -> p b q t", b=MB))
+
+        def reduce_half(h):
+            nc.vector.tensor_reduce(e[:, h * HALF : (h + 1) * HALF, t], last[h][:].rearrange("p (g k) -> p g k", k=K), AX, ADD)
+
+        def quantize_w(b0, b1):
+            nc.vector.quantize_mx(
+                out=w_codes[:, b0:b1, :].rearrange("p b q -> p (b q)").bitcast(X4),
+                scales=w_scales[:, b0:b1, :].rearrange("p b q -> p (b q)"),
+                in_=w_grouped[:, b0:b1, :, :].rearrange("p b q t -> p (b q t)"),
+            )
+
+        def quantize_e(h):
+            s = slice(h * HALF, (h + 1) * HALF)
+            nc.vector.quantize_mx(out=e_codes[:, s].bitcast(X4), scales=e_scales[:, s], in_=e[:, s, :].rearrange("p g t -> p (g t)"))
+
+        reduce_half(0)
+        reduce_half(1)
+        quantize_w(0, 2)
+        quantize_e(0)
+        quantize_w(2, 3)
+        quantize_e(1)
+        for h in range(2):
+            s = slice(h * HALF, (h + 1) * HALF)
+            res = ring.tile([P, MB, HALF], F32, name="res")
+            for b in range(MB):
+                acc = psum.tile([P, HALF], F32, name=f"acc{h}{b}")
+                nc.tensor.matmul_mx(out=acc[:], lhsT=w_codes[:, b, :].bitcast(X4), lhsT_scale=w_scales[:, b, :], rhs=e_codes[:, s].bitcast(X4), rhs_scale=e_scales[:, s], start=True, stop=True)
+                if b == 1:
+                    nc.scalar.activation(res[:, b, :], acc[:], IDENT, bias=bias_col[:, b : b + 1])
+                else:
+                    nc.vector.tensor_scalar(out=res[:, b, :], in0=acc[:], scalar1=bias_col[:, b : b + 1], scalar2=None, op0=ADD)
+            nc.sync.dma_start(out_rows[:, :, s], res[:])

@@ -41,7 +41,7 @@ def tile_attend_grid_bias_kernel(tc, xT, w, part, bias, offs, out):
         x_sb = [keep.tile([P, T], F32, name=f"x{t}") for t in range(PACK)]
         w_sb = [keep.tile([P, PACK, M // 2], F32, name=f"w{c}") for c in range(2)]
 
-        nc.sync.dma_start(part_col[:], part[0:1, :].rearrange("o (p j) -> (o p) j", j=8))
+        nc.scalar.dma_start(part_col[:], part[0:1, :].rearrange("o (p j) -> (o p) j", j=8))
         nc.sync.dma_start(x_sb[0][:], x_planes[0])
         nc.sync.dma_start(offsets[:], offs)
         nc.scalar.dma_start(bias_col[:], bias.rearrange("(q b) o -> q (b o)", b=MB))
@@ -77,7 +77,10 @@ def tile_attend_grid_bias_kernel(tc, xT, w, part, bias, offs, out):
             n = HALF * K
             nc.vector.tensor_tensor(last[h][:], x_sb[t][:].indirect(offsets[:, h * n // 16 : (h + 1) * n // 16]), part_row[:, h * n : (h + 1) * n], MULT)
         for c in range(2):
-            nc.scalar.copy(out=w_grouped[:, :, 64 * c : 64 * c + 64, :], in_=w_sb[c][:].rearrange("p t (q b) -> p b q t", b=MB))
+            nc.scalar.copy(
+                out=w_grouped[:, :, 64 * c : 64 * c + 64, :].rearrange("p b q t -> p q b t"),
+                in_=w_sb[c][:].rearrange("p t (q b) -> p q b t", b=MB),
+            )
 
         def reduce_half(h):
             nc.vector.tensor_reduce(e[:, h * HALF : (h + 1) * HALF, t], last[h][:].rearrange("p (g k) -> p g k", k=K), AX, ADD)
@@ -99,14 +102,15 @@ def tile_attend_grid_bias_kernel(tc, xT, w, part, bias, offs, out):
         quantize_e(0)
         quantize_w(2, 3)
         quantize_e(1)
+        queues = (nc.sync, nc.scalar, nc.sync)
         for h in range(2):
             s = slice(h * HALF, (h + 1) * HALF)
-            res = ring.tile([P, MB, HALF], F32, name="res")
             for b in range(MB):
                 acc = psum.tile([P, HALF], F32, name=f"acc{h}{b}")
                 nc.tensor.matmul_mx(out=acc[:], lhsT=w_codes[:, b, :].bitcast(X4), lhsT_scale=w_scales[:, b, :], rhs=e_codes[:, s].bitcast(X4), rhs_scale=e_scales[:, s], start=True, stop=True)
+                res = keep.tile([P, HALF], F32, name=f"res{h}{b}")
                 if b == 1:
-                    nc.scalar.activation(res[:, b, :], acc[:], IDENT, bias=bias_col[:, b : b + 1])
+                    nc.scalar.activation(res[:], acc[:], IDENT, bias=bias_col[:, b : b + 1])
                 else:
-                    nc.vector.tensor_scalar(out=res[:, b, :], in0=acc[:], scalar1=bias_col[:, b : b + 1], scalar2=None, op0=ADD)
-            nc.sync.dma_start(out_rows[:, :, s], res[:])
+                    nc.vector.tensor_scalar(out=res[:], in0=acc[:], scalar1=bias_col[:, b : b + 1], scalar2=None, op0=ADD)
+                queues[b].dma_start(out_rows[:, b, s], res[:])

from contextlib import ExitStack

import concourse.mybir as mybir
from concourse.masks import make_identity

D, T, M, G, K = 512, 4096, 384, 256, 4
P, PACK = 128, 4
HALF = 128
MB = M // P

F32 = mybir.dt.float32
BF16 = mybir.dt.bfloat16
U32 = mybir.dt.uint32
U16 = mybir.dt.uint16
U8 = mybir.dt.uint8
X4 = mybir.dt.float8_e4m3fn_x4
ADD = mybir.AluOpType.add
MULT = mybir.AluOpType.mult
AX = mybir.AxisListType.X
IDENT = mybir.ActivationFunctionType.Identity

FLOPS = 2 * D * M * G
BYTES = 4 * (D * T + D * M + G * K + M + M * G) + 2 * P * (G * K // 16)


def tile_attend_grid_bias_kernel(tc, xT, w, part, bias, offs, out):
    nc = tc.nc
    x_planes = xT.rearrange("(p t) c -> t p c", t=PACK)
    w_planes = w.rearrange("(p t) m -> p t m", t=PACK)
    out_rows = out.rearrange("(q b) g -> q b g", b=MB)
    with ExitStack() as ctx:
        ctx.enter_context(nc.allow_low_precision("sums are rounded once to bfloat16"))
        lists = ctx.enter_context(tc.tile_pool(name="lists", bufs=1))
        keep = ctx.enter_context(tc.tile_pool(name="keep", bufs=1))
        ring = ctx.enter_context(tc.tile_pool(name="ring", bufs=2))
        psum = ctx.enter_context(tc.psum_pool(name="psum", bufs=1))

        offsets = lists.tile([P, G * K // 16], U16, name="offsets")
        part_col = keep.tile([P, 8], F32, name="part_col")
        bias_col = keep.tile([P, MB], F32, name="bias_col")
        x_sb = [keep.tile([P, T], F32, name=f"x{t}") for t in range(PACK)]
        w_sb = [keep.tile([P, PACK, M // 2], F32, name=f"w{c}") for c in range(2)]

        nc.scalar.dma_start(part_col[:], part[0:1, :].rearrange("o (p j) -> (o p) j", j=8))
        nc.sync.dma_start(x_sb[0][:], x_planes[0])
        nc.sync.dma_start(offsets[:], offs)
        nc.scalar.dma_start(bias_col[:], bias.rearrange("(q b) o -> q (b o)", b=MB))
        for t in range(1, PACK):
            nc.sync.dma_start(x_sb[t][:], x_planes[t])
        for c in range(2):
            nc.sync.dma_start(w_sb[c][:], w_planes[:, :, c * (M // 2) : (c + 1) * (M // 2)])

        ident = keep.tile([P, P], F32, name="ident")
        make_identity(nc, ident[:])
        part_sb = keep.tile([P, P, 8], F32, name="part_sb")
        for h in range(2):
            pt = psum.tile([P, 4, P], F32, name=f"pt{h}")
            for j in range(4):
                nc.tensor.transpose(pt[:, j, :], part_col[:, 4 * h + j : 4 * h + j + 1].to_broadcast([P, P]), ident[:])
            nc.scalar.copy(out=part_sb[:, :, 4 * h : 4 * h + 4], in_=pt[:].rearrange("p j a -> p a j"))
        part_row = part_sb[:].rearrange("p a j -> p (a j)")

        e = keep.tile([P, G, PACK], BF16, name="e", align_bytes=64)
        for t in range(PACK - 1):
            prod = ring.tile([P, G * K], F32, name="prod")
            nc.vector.tensor_tensor(prod[:], x_sb[t][:].indirect(offsets[:]), part_row, MULT)
            nc.vector.tensor_reduce(e[:, :, t], prod[:].rearrange("p (g k) -> p g k", k=K), AX, ADD)

        w_grouped = keep.tile([P, MB, P, PACK], BF16, name="w_grouped", align_bytes=64)
        w_codes = keep.tile([P, MB, P], U32, name="w_codes", align_bytes=64)
        w_scales = keep.tile([P, MB, P], U8, name="w_scales", align_bytes=64)
        e_codes = keep.tile([P, G], U32, name="e_codes", align_bytes=64)
        e_scales = keep.tile([P, G], U8, name="e_scales", align_bytes=64)
        t = PACK - 1
        last = [ring.tile([P, HALF * K], F32, name=f"last{h}") for h in range(2)]
        for h in range(2):
            n = HALF * K
            nc.vector.tensor_tensor(last[h][:], x_sb[t][:].indirect(offsets[:, h * n // 16 : (h + 1) * n // 16]), part_row[:, h * n : (h + 1) * n], MULT)
        for c in range(2):
            nc.scalar.copy(
                out=w_grouped[:, :, 64 * c : 64 * c + 64, :].rearrange("p b q t -> p q b t"),
                in_=w_sb[c][:].rearrange("p t (q b) -> p q b t", b=MB),
            )

        def reduce_half(h):
            nc.vector.tensor_reduce(e[:, h * HALF : (h + 1) * HALF, t], last[h][:].rearrange("p (g k) -> p g k", k=K), AX, ADD)

        def quantize_w(b0, b1):
            nc.vector.quantize_mx(
                out=w_codes[:, b0:b1, :].rearrange("p b q -> p (b q)").bitcast(X4),
                scales=w_scales[:, b0:b1, :].rearrange("p b q -> p (b q)"),
                in_=w_grouped[:, b0:b1, :, :].rearrange("p b q t -> p (b q t)"),
            )

        def quantize_e(h):
            s = slice(h * HALF, (h + 1) * HALF)
            nc.vector.quantize_mx(out=e_codes[:, s].bitcast(X4), scales=e_scales[:, s], in_=e[:, s, :].rearrange("p g t -> p (g t)"))

        reduce_half(0)
        reduce_half(1)
        quantize_w(0, 2)
        quantize_e(0)
        quantize_w(2, 3)
        quantize_e(1)
        queues = (nc.sync, nc.scalar, nc.sync)
        for h in range(2):
            s = slice(h * HALF, (h + 1) * HALF)
            for b in range(MB):
                acc = psum.tile([P, HALF], F32, name=f"acc{h}{b}")
                nc.tensor.matmul_mx(out=acc[:], lhsT=w_codes[:, b, :].bitcast(X4), lhsT_scale=w_scales[:, b, :], rhs=e_codes[:, s].bitcast(X4), rhs_scale=e_scales[:, s], start=True, stop=True)
                res = keep.tile([P, HALF], F32, name=f"res{h}{b}")
                if b == 1:
                    nc.scalar.activation(res[:], acc[:], IDENT, bias=bias_col[:, b : b + 1])
                else:
                    nc.vector.tensor_scalar(out=res[:], in0=acc[:], scalar1=bias_col[:, b : b + 1], scalar2=None, op0=ADD)
                queues[b].dma_start(out_rows[:, b, s], res[:])
